import numpy as np
import ml_dtypes


def mxq(x, axis, fmt="e4m3"):
    dtype, down = {"e4m3": (ml_dtypes.float8_e4m3fn, 7), "e5m2": (ml_dtypes.float8_e5m2, 14)}[fmt]
    v = np.moveaxis(np.asarray(x, np.float32).astype(ml_dtypes.bfloat16).astype(np.float64), axis, -1)
    blocks = v.reshape(v.shape[:-1] + (-1, 32))
    amax = np.abs(blocks).max(-1, keepdims=True)
    byte = np.maximum(np.where(amax > 0, np.frexp(amax)[1] - 1 + 127, 0) - down, 1)
    scale = np.exp2(byte - 127.0)
    codes = (blocks / scale).astype(np.float32).astype(dtype).astype(np.float64)
    return np.moveaxis((codes * scale).reshape(v.shape), -1, axis)


WIDE = False


def mx_kscale(k):
    if not WIDE:
        return np.ones(k)
    levels = np.array([10, -10, 5, -5, 0])
    if k % 512:
        return np.exp2(np.random.permutation(np.resize(levels, k // 32))).repeat(32)
    a = np.empty((k // 512, 16))
    for p in range(k // 512):
        a[p, :8] = np.random.permutation(np.resize(levels, 8))
        for g in range(8):
            far = levels[np.abs(levels - a[p, g]) >= 10]
            a[p, g + 8] = far[np.random.randint(len(far))]
    return np.exp2(a.ravel()).repeat(32)


def f64(x):
    return np.asarray(x).astype(np.float64)


def striped(idx):
    return np.tile(idx.reshape(-1, 16).T, (8, 1)).astype(np.uint16)


def unstriped(offs):
    return offs[:16].T.reshape(-1).astype(np.int64)


def pack_weight(w):
    k, n = w.shape
    w = f64(np.asarray(w, np.float32).astype(ml_dtypes.bfloat16)).reshape(k // 32, 32, n)
    amax = np.abs(w).max(1)
    byte = np.clip(np.where(amax > 0, np.frexp(amax)[1] - 1 + 127 - 7, 1), 1, 254)
    scaled = (w * np.exp2(127.0 - byte)[:, None, :]).reshape(k, n).astype(np.float32)
    words = np.ascontiguousarray(scaled.reshape(k // 512, 128, 4, n).transpose(0, 1, 3, 2)).astype(ml_dtypes.float8_e4m3fn).view(np.uint8)
    return words, np.ascontiguousarray(byte.astype(np.uint8).reshape(k // 512, 16, n))


def unpack_weight(words, scales):
    g, p, n, _ = words.shape
    vals = np.ascontiguousarray(words).view(ml_dtypes.float8_e4m3fn).astype(np.float64) * np.repeat(np.exp2(scales.astype(np.float64) - 127.0), 8, axis=1)[..., None]
    return vals.transpose(0, 1, 3, 2).reshape(g * 512, n)


def sigmoid(v):
    return 1.0 / (1.0 + np.exp(-np.maximum(v, -700.0)))


K, T, S, N, W = 512, 1024, 512, 128, 2048


def setup_inputs():
    n = np.random.standard_normal
    s = mx_kscale(K)[:, None]
    packed_xT = pack_weight(n((K, T)) * s)
    packed_eT = pack_weight(n((K, W)) * s)
    return {
        "x_words": packed_xT[0],
        "x_scales": packed_xT[1],
        "e_words": packed_eT[0],
        "e_scales": packed_eT[1],
        "w1": (n((K, N)) / np.sqrt(K) / s).astype(np.float32),
        "w2": (n((K, N)) / np.sqrt(K) / s).astype(np.float32),
        "theta": (n((N, 4))).astype(np.float32),
        "offs": striped(np.random.permutation(T)[:S]),
        "item": striped(np.random.permutation(W)[:S]),
    }


def reference(x_words, x_scales, e_words, e_scales, w1, w2, theta, offs, item):
    xq = unpack_weight(x_words, x_scales)[:, unstriped(offs)]
    a = sigmoid(mxq(f64(w1), 0, "e4m3").T @ xq)
    e_item = unpack_weight(e_words, e_scales)[:, unstriped(item)]
    p = sigmoid(mxq(f64(w2), 0, "e4m3").T @ e_item)
    ap = a * p
    a0 = a - ap
    p0 = p - ap
    c0 = ap - a - p + 1.0
    return np.tanh(f64(theta)[:, 1:2] * a0 + f64(theta)[:, 2:3] * p0 + f64(theta)[:, 3:4] * ap + f64(theta)[:, 0:1] * c0)

@@ -1,0 +1,147 @@
+from contextlib import ExitStack
+
+import concourse.mybir as mybir
+
+F32 = mybir.dt.float32
+BF16 = mybir.dt.bfloat16
+I32 = mybir.dt.int32
+U32 = mybir.dt.uint32
+U16 = mybir.dt.uint16
+U8 = mybir.dt.uint8
+FP8X4 = mybir.dt.float8_e4m3fn_x4
+ALU = mybir.AluOpType
+ACT = mybir.ActivationFunctionType
+
+P = 128
+PACK = 4
+K, T, S, N, W = 512, 1024, 512, 128, 2048
+HALF = S // 2
+FLOPS = 2 * 2 * K * N * S
+
+
+def tile_picked_ylatt_tanh_p_kernel(
+    tc, x_words, x_scales, e_words, e_scales, w1, w2, theta, offs, item, out
+):
+    nc = tc.nc
+    with ExitStack() as ctx:
+        keep = ctx.enter_context(tc.tile_pool(name="keep", bufs=1))
+        psum = ctx.enter_context(tc.psum_pool(name="psum", bufs=1))
+
+        offs_sb = keep.tile([P, S // 16], U16, name="offs_sb")
+        item_sb = keep.tile([P, S // 16], U16, name="item_sb")
+        x_word_table = keep.tile([P, T], I32, name="x_word_table", align_bytes=64)
+        e_word_table = keep.tile([P, W], I32, name="e_word_table", align_bytes=64)
+        x_scale_table = keep.tile([P, T], U8, name="x_scale_table", align_bytes=64)
+        e_scale_table = keep.tile([P, W], U8, name="e_scale_table", tag="e_reused", align_bytes=64)
+        w1_raw = keep.tile([P, PACK, N], F32, name="w1_raw")
+        w2_raw = keep.tile([P, PACK, N], F32, name="w2_raw")
+        theta_sb = keep.tile([P, 4], F32, name="theta_sb")
+
+        def load_scales(queues, table, scales, first):
+            for q, queue in queues:
+                row = 32 * q + first
+                queue.dma_start(
+                    out=table[row : row + 4, :].bitcast(I32),
+                    in_=scales[0, 4 * q : 4 * q + 4, :].bitcast(I32),
+                )
+
+        def load_words(queue, table, words):
+            queue.dma_start(out=table[:], in_=words[0].rearrange("p c r -> p (c r)").bitcast(I32))
+
+        def load_weight(queue, raw, w):
+            queue.dma_start(out=raw[:], in_=w.rearrange("(p j) n -> p j n", j=PACK))
+
+        nc.vector.memset(x_scale_table[:].bitcast(I32), 0)
+        nc.vector.memset(e_scale_table[:].bitcast(I32), 0)
+        signs = keep.tile([P, 4, 4], F32, name="signs")
+        nc.vector.memset(signs[:], 0.25)
+        nc.vector.memset(signs[:, 1, 0:4:2], -0.25)
+        nc.vector.memset(signs[:, 2, 0:2], -0.25)
+        nc.vector.memset(signs[:, 3, 1:3], -0.25)
+        nc.sync.dma_start(offs_sb[:], offs)
+        nc.sync.dma_start(item_sb[:], item)
+        load_words(nc.scalar, x_word_table, x_words)
+        load_words(nc.scalar, e_word_table, e_words)
+        load_scales([(q, nc.sync) for q in range(4)], x_scale_table, x_scales, 0)
+        load_scales([(q, nc.sync) for q in range(3)], e_scale_table, e_scales, 4)
+        nc.gpsimd.dma_start(out=theta_sb[:], in_=theta)
+        load_weight(nc.gpsimd, w1_raw, w1)
+        load_weight(nc.gpsimd, w2_raw, w2)
+        load_scales([(3, nc.gpsimd)], e_scale_table, e_scales, 4)
+
+        signed = keep.tile([P, 4, 4], F32, name="signed")
+        coef = keep.tile([P, 4], F32, name="coef")
+        nc.vector.tensor_tensor(signed[:], signs[:], theta_sb[:].unsqueeze(1).to_broadcast([P, 4, 4]), ALU.mult)
+        nc.vector.tensor_reduce(coef[:], signed[:], mybir.AxisListType.X, ALU.add)
+        c_one, c_a, c_b, c_ab = (coef[:, i : i + 1] for i in range(4))
+
+        def group_weight(raw, name):
+            grouped = keep.tile([P, N, PACK], BF16, name=name, align_bytes=64)
+            nc.scalar.activation(grouped[:], raw[:].rearrange("p j n -> p n j"), ACT.Identity)
+            return grouped
+
+        def quantise(grouped, name):
+            codes = keep.tile([P, N], U32, name=name + "_codes", align_bytes=64)
+            scales = keep.tile([P, N], U8, name=name + "_scales", align_bytes=64)
+            nc.vector.quantize_mx(
+                out=codes[:].bitcast(FP8X4), scales=scales[:], in_=grouped[:].rearrange("p n j -> p (n j)")
+            )
+            return codes, scales
+
+        w1_grouped = group_weight(w1_raw, "w1_grouped")
+        w2_grouped = group_weight(w2_raw, "w2_grouped")
+
+        x_scale_picked = keep.tile([P, S], U8, name="x_scale_picked", align_bytes=64)
+        x_word_picked = keep.tile([P, S], U32, name="x_word_picked", align_bytes=64)
+        e_scale_picked = keep.tile([P, S], U8, name="e_scale_picked", align_bytes=64)
+        nc.vector.tensor_copy(x_scale_picked[:], x_scale_table[:].indirect(offs_sb[:]))
+        nc.vector.tensor_copy(x_word_picked[:], x_word_table[:].bitcast(U32).indirect(offs_sb[:]))
+        w1_codes, w1_scales = quantise(w1_grouped, "w1")
+        nc.vector.tensor_copy(e_scale_picked[:], e_scale_table[:].indirect(item_sb[:]))
+        w2_codes, w2_scales = quantise(w2_grouped, "w2")
+
+        a_sums = psum.tile([N, S], F32, name="a_sums")
+        nc.tensor.matmul_mx(
+            out=a_sums[:],
+            lhsT=w1_codes[:].bitcast(FP8X4),
+            lhsT_scale=w1_scales[:],
+            rhs=x_word_picked[:].bitcast(FP8X4),
+            rhs_scale=x_scale_picked[0:P, :],
+            start=True,
+            stop=True,
+        )
+        a_tanh = keep.tile([N, S], F32, name="a_tanh")
+        slope = keep.tile([N, S], F32, name="slope")
+        nc.scalar.activation(a_tanh[:], a_sums[:], ACT.Tanh, scale=0.5)
+        nc.scalar.activation(slope[:], a_tanh[:], ACT.Identity, scale=c_ab, bias=c_b)
+
+        b_tanh = []
+        for h in range(2):
+            cols = slice(h * HALF, (h + 1) * HALF)
+            picked = keep.tile([P, HALF], U32, name="e_word_picked%d" % h, tag=("e_reused", "e_second")[h], align_bytes=64)
+            nc.vector.tensor_copy(
+                picked[:], e_word_table[:].bitcast(U32).indirect(item_sb[:, h * HALF // 16 : (h + 1) * HALF // 16])
+            )
+            b_sums = psum.tile([N, HALF], F32, name="b_sums%d" % h)
+            nc.tensor.matmul_mx(
+                out=b_sums[:],
+                lhsT=w2_codes[:].bitcast(FP8X4),
+                lhsT_scale=w2_scales[:],
+                rhs=picked[:].bitcast(FP8X4),
+                rhs_scale=e_scale_picked[4:P, cols],
+                start=True,
+                stop=True,
+            )
+            b_half = keep.tile([N, HALF], F32, name="b_tanh%d" % h)
+            nc.scalar.activation(b_half[:], b_sums[:], ACT.Tanh, scale=0.5)
+            b_tanh.append(b_half)
+
+        for h in range(2):
+            cols = slice(h * HALF, (h + 1) * HALF)
+            product = keep.tile([N, HALF], F32, name="product%d" % h)
+            lattice = keep.tile([N, HALF], F32, name="lattice%d" % h)
+            result = keep.tile([N, HALF], F32, name="result%d" % h)
+            nc.vector.tensor_tensor(product[:], b_tanh[h][:], slope[:, cols], ALU.mult)
+            nc.vector.scalar_tensor_tensor(lattice[:], a_tanh[:, cols], c_a, product[:], ALU.mult, ALU.add)
+            nc.scalar.activation(result[:], lattice[:], ACT.Tanh, bias=c_one)
+            nc.sync.dma_start(out=out[:, cols], in_=result[:])

@@ -16,6 +16,7 @@ P = 128
 PACK = 4
 K, T, S, N, W = 512, 1024, 512, 128, 2048
 HALF = S // 2
+PIECE = 128
 FLOPS = 2 * 2 * K * N * S
 
 
@@ -32,7 +33,7 @@ def tile_picked_ylatt_tanh_p_kernel(
         x_word_table = keep.tile([P, T], I32, name="x_word_table", align_bytes=64)
         e_word_table = keep.tile([P, W], I32, name="e_word_table", align_bytes=64)
         x_scale_table = keep.tile([P, T], U8, name="x_scale_table", align_bytes=64)
-        e_scale_table = keep.tile([P, W], U8, name="e_scale_table", tag="e_reused", align_bytes=64)
+        e_scale_table = keep.tile([P, W], U8, name="e_scale_table", align_bytes=64)
         w1_raw = keep.tile([P, PACK, N], F32, name="w1_raw")
         w2_raw = keep.tile([P, PACK, N], F32, name="w2_raw")
         theta_sb = keep.tile([P, 4], F32, name="theta_sb")
@@ -58,16 +59,15 @@ def tile_picked_ylatt_tanh_p_kernel(
         nc.vector.memset(signs[:, 1, 0:4:2], -0.25)
         nc.vector.memset(signs[:, 2, 0:2], -0.25)
         nc.vector.memset(signs[:, 3, 1:3], -0.25)
+        nc.scalar.dma_start(out=theta_sb[:], in_=theta)
         nc.sync.dma_start(offs_sb[:], offs)
         nc.sync.dma_start(item_sb[:], item)
-        load_words(nc.scalar, x_word_table, x_words)
-        load_words(nc.scalar, e_word_table, e_words)
-        load_scales([(q, nc.sync) for q in range(4)], x_scale_table, x_scales, 0)
-        load_scales([(q, nc.sync) for q in range(3)], e_scale_table, e_scales, 4)
-        nc.gpsimd.dma_start(out=theta_sb[:], in_=theta)
-        load_weight(nc.gpsimd, w1_raw, w1)
-        load_weight(nc.gpsimd, w2_raw, w2)
-        load_scales([(3, nc.gpsimd)], e_scale_table, e_scales, 4)
+        load_scales([(0, nc.sync), (1, nc.sync), (2, nc.scalar), (3, nc.scalar)], x_scale_table, x_scales, 0)
+        load_words(nc.sync, x_word_table, x_words)
+        load_weight(nc.sync, w1_raw, w1)
+        load_weight(nc.sync, w2_raw, w2)
+        load_scales([(q, nc.sync) for q in range(4)], e_scale_table, e_scales, 4)
+        load_words(nc.sync, e_word_table, e_words)
 
         signed = keep.tile([P, 4, 4], F32, name="signed")
         coef = keep.tile([P, 4], F32, name="coef")
@@ -75,8 +75,8 @@ def tile_picked_ylatt_tanh_p_kernel(
         nc.vector.tensor_reduce(coef[:], signed[:], mybir.AxisListType.X, ALU.add)
         c_one, c_a, c_b, c_ab = (coef[:, i : i + 1] for i in range(4))
 
-        def group_weight(raw, name):
-            grouped = keep.tile([P, N, PACK], BF16, name=name, align_bytes=64)
+        def group_weight(raw, name, tag):
+            grouped = keep.tile([P, N, PACK], BF16, name=name, tag=tag, align_bytes=64)
             nc.scalar.activation(grouped[:], raw[:].rearrange("p j n -> p n j"), ACT.Identity)
             return grouped
 
@@ -88,8 +88,8 @@ def tile_picked_ylatt_tanh_p_kernel(
             )
             return codes, scales
 
-        w1_grouped = group_weight(w1_raw, "w1_grouped")
-        w2_grouped = group_weight(w2_raw, "w2_grouped")
+        w1_grouped = group_weight(w1_raw, "w1_grouped", "w1_grouped")
+        w2_grouped = group_weight(w2_raw, "w2_grouped", "w2_grouped")
 
         x_scale_picked = keep.tile([P, S], U8, name="x_scale_picked", align_bytes=64)
         x_word_picked = keep.tile([P, S], U32, name="x_word_picked", align_bytes=64)
@@ -117,31 +117,36 @@ def tile_picked_ylatt_tanh_p_kernel(
 
         b_tanh = []
         for h in range(2):
-            cols = slice(h * HALF, (h + 1) * HALF)
-            picked = keep.tile([P, HALF], U32, name="e_word_picked%d" % h, tag=("e_reused", "e_second")[h], align_bytes=64)
+            picked = keep.tile([P, HALF], U32, name="e_word_picked%d" % h, align_bytes=64)
             nc.vector.tensor_copy(
                 picked[:], e_word_table[:].bitcast(U32).indirect(item_sb[:, h * HALF // 16 : (h + 1) * HALF // 16])
             )
-            b_sums = psum.tile([N, HALF], F32, name="b_sums%d" % h)
-            nc.tensor.matmul_mx(
-                out=b_sums[:],
-                lhsT=w2_codes[:].bitcast(FP8X4),
-                lhsT_scale=w2_scales[:],
-                rhs=picked[:].bitcast(FP8X4),
-                rhs_scale=e_scale_picked[4:P, cols],
-                start=True,
-                stop=True,
-            )
-            b_half = keep.tile([N, HALF], F32, name="b_tanh%d" % h)
-            nc.scalar.activation(b_half[:], b_sums[:], ACT.Tanh, scale=0.5)
-            b_tanh.append(b_half)
+            for u in range(HALF // PIECE):
+                first = h * HALF + u * PIECE
+                b_sums = psum.tile([N, PIECE], F32, name="b_sums%d" % first)
+                nc.tensor.matmul_mx(
+                    out=b_sums[:],
+                    lhsT=w2_codes[:].bitcast(FP8X4),
+                    lhsT_scale=w2_scales[:],
+                    rhs=picked[:, u * PIECE : (u + 1) * PIECE].bitcast(FP8X4),
+                    rhs_scale=e_scale_picked[4:P, first : first + PIECE],
+                    start=True,
+                    stop=True,
+                )
+                b_piece = keep.tile([N, PIECE], F32, name="b_tanh%d" % first)
+                nc.scalar.activation(b_piece[:], b_sums[:], ACT.Tanh, scale=0.5)
+                b_tanh.append(b_piece)
 
-        for h in range(2):
-            cols = slice(h * HALF, (h + 1) * HALF)
-            product = keep.tile([N, HALF], F32, name="product%d" % h)
-            lattice = keep.tile([N, HALF], F32, name="lattice%d" % h)
-            result = keep.tile([N, HALF], F32, name="result%d" % h)
-            nc.vector.tensor_tensor(product[:], b_tanh[h][:], slope[:, cols], ALU.mult)
-            nc.vector.scalar_tensor_tensor(lattice[:], a_tanh[:, cols], c_a, product[:], ALU.mult, ALU.add)
-            nc.scalar.activation(result[:], lattice[:], ACT.Tanh, bias=c_one)
-            nc.sync.dma_start(out=out[:, cols], in_=result[:])
+        for pair in range(0, S // PIECE, 2):
+            products = []
+            for i in (pair, pair + 1):
+                product = keep.tile([N, PIECE], F32, name="product%d" % i)
+                nc.vector.tensor_tensor(product[:], b_tanh[i][:], slope[:, i * PIECE : (i + 1) * PIECE], ALU.mult)
+                products.append(product)
+            for i in (pair, pair + 1):
+                cols = slice(i * PIECE, (i + 1) * PIECE)
+                lattice = keep.tile([N, PIECE], F32, name="lattice%d" % i)
+                result = keep.tile([N, PIECE], F32, name="result%d" % i)
+                nc.vector.scalar_tensor_tensor(lattice[:], a_tanh[:, cols], c_a, products[i - pair][:], ALU.mult, ALU.add)
+                nc.scalar.activation(result[:], lattice[:], ACT.Tanh, bias=c_one)
+                nc.sync.dma_start(out=out[:, cols], in_=result[:])

@@ -40,10 +40,9 @@ def tile_picked_ylatt_tanh_p_kernel(
 
         def load_scales(queues, table, scales, first):
             for q, queue in queues:
-                row = 32 * q + first
                 queue.dma_start(
-                    out=table[row : row + 4, :].bitcast(I32),
-                    in_=scales[0, 4 * q : 4 * q + 4, :].bitcast(I32),
+                    out=table[:].bitcast(I32)[first + q : P : 32, :],
+                    in_=scales[0].bitcast(I32)[q : 16 : 4, :],
                 )
 
         def load_words(queue, table, words):

@@ -38,41 +38,43 @@ def tile_picked_ylatt_tanh_p_kernel(
         w2_raw = keep.tile([P, PACK, N], F32, name="w2_raw")
         theta_sb = keep.tile([P, 4], F32, name="theta_sb")
 
-        def load_scales(queues, table, scales, first):
-            for q, queue in queues:
-                queue.dma_start(
-                    out=table[:].bitcast(I32)[first + q : P : 32, :],
-                    in_=scales[0].bitcast(I32)[q : 16 : 4, :],
-                )
+        def load_scales(queue, table, scales):
+            queue.dma_start(out=table[:].bitcast(I32)[0:P:8, :], in_=scales[0].bitcast(I32))
 
-        def load_words(queue, table, words):
-            queue.dma_start(out=table[:], in_=words[0].rearrange("p c r -> p (c r)").bitcast(I32))
+        def place_scales(queue, plane, picked):
+            for r in range(4):
+                queue.dma_start(out=plane[:].bitcast(I32)[r:P:32, :], in_=picked[:].bitcast(I32)[8 * r : P : 32, :])
+
+        def load_words(queue, table, words, lo, hi):
+            queue.dma_start(out=table[:, lo:hi], in_=words[0].rearrange("p c r -> p (c r)").bitcast(I32)[:, lo:hi])
 
         def load_weight(queue, raw, w):
             queue.dma_start(out=raw[:], in_=w.rearrange("(p j) n -> p j n", j=PACK))
 
         nc.vector.memset(x_scale_table[:].bitcast(I32), 0)
-        nc.vector.memset(e_scale_table[:].bitcast(I32), 0)
-        signs = keep.tile([P, 4, 4], F32, name="signs")
-        nc.vector.memset(signs[:], 0.25)
-        nc.vector.memset(signs[:, 1, 0:4:2], -0.25)
-        nc.vector.memset(signs[:, 2, 0:2], -0.25)
-        nc.vector.memset(signs[:, 3, 1:3], -0.25)
+        nc.gpsimd.memset(e_scale_table[:].bitcast(I32), 0)
+        x_plane = keep.tile([P, S], U8, name="x_plane", align_bytes=64)
+        e_plane = keep.tile([P, S], U8, name="e_plane", align_bytes=64)
+        nc.vector.memset(x_plane[:].bitcast(I32), 0)
+        nc.vector.memset(e_plane[:].bitcast(I32), 0)
         nc.scalar.dma_start(out=theta_sb[:], in_=theta)
         nc.sync.dma_start(offs_sb[:], offs)
         nc.sync.dma_start(item_sb[:], item)
-        load_scales([(0, nc.sync), (1, nc.sync), (2, nc.scalar), (3, nc.scalar)], x_scale_table, x_scales, 0)
-        load_words(nc.sync, x_word_table, x_words)
+        load_scales(nc.sync, x_scale_table, x_scales)
+        load_scales(nc.sync, e_scale_table, e_scales)
+        load_words(nc.sync, x_word_table, x_words, 0, T)
         load_weight(nc.sync, w1_raw, w1)
         load_weight(nc.sync, w2_raw, w2)
-        load_scales([(q, nc.sync) for q in range(4)], e_scale_table, e_scales, 4)
-        load_words(nc.sync, e_word_table, e_words)
+        load_words(nc.sync, e_word_table, e_words, 0, W)
 
-        signed = keep.tile([P, 4, 4], F32, name="signed")
-        coef = keep.tile([P, 4], F32, name="coef")
-        nc.vector.tensor_tensor(signed[:], signs[:], theta_sb[:].unsqueeze(1).to_broadcast([P, 4, 4]), ALU.mult)
-        nc.vector.tensor_reduce(coef[:], signed[:], mybir.AxisListType.X, ALU.add)
-        c_one, c_a, c_b, c_ab = (coef[:, i : i + 1] for i in range(4))
+        terms = keep.tile([P, 5, 4], F32, name="terms")
+        coef = keep.tile([P, 5], F32, name="coef")
+        c_one, c_a, c_b, c_ab, shift = (coef[:, i : i + 1] for i in range(5))
+        nc.scalar.activation(terms[:, 0, :], theta_sb[:], ACT.Identity, scale=-0.125, accum_out=shift)
+        nc.scalar.activation(terms[:, 1, :], theta_sb[:], ACT.Identity, scale=0.25, accum_out=c_one)
+        nc.scalar.activation(terms[:, 2, 0:2], theta_sb[:, 1:4:2], ACT.Identity, scale=0.5, bias=shift, accum_out=c_a)
+        nc.scalar.activation(terms[:, 3, 0:2], theta_sb[:, 2:4], ACT.Identity, scale=0.5, bias=shift, accum_out=c_b)
+        nc.scalar.activation(terms[:, 4, 0:2], theta_sb[:, 0:4:3], ACT.Identity, scale=0.5, bias=shift, accum_out=c_ab)
 
         def group_weight(raw, name, tag):
             grouped = keep.tile([P, N, PACK], BF16, name=name, tag=tag, align_bytes=64)
@@ -94,25 +96,28 @@ def tile_picked_ylatt_tanh_p_kernel(
         x_word_picked = keep.tile([P, S], U32, name="x_word_picked", align_bytes=64)
         e_scale_picked = keep.tile([P, S], U8, name="e_scale_picked", align_bytes=64)
         nc.vector.tensor_copy(x_scale_picked[:], x_scale_table[:].indirect(offs_sb[:]))
+        place_scales(nc.scalar, x_plane, x_scale_picked)
+        nc.vector.tensor_copy(e_scale_picked[:], e_scale_table[:].indirect(item_sb[:]))
+        place_scales(nc.sync, e_plane, e_scale_picked)
         nc.vector.tensor_copy(x_word_picked[:], x_word_table[:].bitcast(U32).indirect(offs_sb[:]))
         w1_codes, w1_scales = quantise(w1_grouped, "w1")
-        nc.vector.tensor_copy(e_scale_picked[:], e_scale_table[:].indirect(item_sb[:]))
         w2_codes, w2_scales = quantise(w2_grouped, "w2")
 
-        a_sums = psum.tile([N, S], F32, name="a_sums")
-        nc.tensor.matmul_mx(
-            out=a_sums[:],
-            lhsT=w1_codes[:].bitcast(FP8X4),
-            lhsT_scale=w1_scales[:],
-            rhs=x_word_picked[:].bitcast(FP8X4),
-            rhs_scale=x_scale_picked[0:P, :],
-            start=True,
-            stop=True,
-        )
         a_tanh = keep.tile([N, S], F32, name="a_tanh")
         slope = keep.tile([N, S], F32, name="slope")
-        nc.scalar.activation(a_tanh[:], a_sums[:], ACT.Tanh, scale=0.5)
-        nc.scalar.activation(slope[:], a_tanh[:], ACT.Identity, scale=c_ab, bias=c_b)
+        for lo in range(0, S, HALF):
+            a_sums = psum.tile([N, HALF], F32, name="a_sums%d" % lo)
+            nc.tensor.matmul_mx(
+                out=a_sums[:],
+                lhsT=w1_codes[:].bitcast(FP8X4),
+                lhsT_scale=w1_scales[:],
+                rhs=x_word_picked[:, lo : lo + HALF].bitcast(FP8X4),
+                rhs_scale=x_plane[:, lo : lo + HALF],
+                start=True,
+                stop=True,
+            )
+            nc.scalar.activation(a_tanh[:, lo : lo + HALF], a_sums[:], ACT.Tanh, scale=0.5)
+            nc.scalar.activation(slope[:, lo : lo + HALF], a_tanh[:, lo : lo + HALF], ACT.Identity, scale=c_ab, bias=c_b)
 
         b_tanh = []
         for h in range(2):
@@ -128,7 +133,7 @@ def tile_picked_ylatt_tanh_p_kernel(
                     lhsT=w2_codes[:].bitcast(FP8X4),
                     lhsT_scale=w2_scales[:],
                     rhs=picked[:, u * PIECE : (u + 1) * PIECE].bitcast(FP8X4),
-                    rhs_scale=e_scale_picked[4:P, first : first + PIECE],
+                    rhs_scale=e_plane[:, first : first + PIECE],
                     start=True,
                     stop=True,
                 )

@@ -33,17 +33,21 @@ def tile_picked_ylatt_tanh_p_kernel(
         x_word_table = keep.tile([P, T], I32, name="x_word_table", align_bytes=64)
         e_word_table = keep.tile([P, W], I32, name="e_word_table", align_bytes=64)
         x_scale_table = keep.tile([P, T], U8, name="x_scale_table", align_bytes=64)
-        e_scale_table = keep.tile([P, W], U8, name="e_scale_table", align_bytes=64)
+        e_scale_table = keep.tile([P, W], U8, name="e_scale_table", tag="held", align_bytes=64)
         w1_raw = keep.tile([P, PACK, N], F32, name="w1_raw")
         w2_raw = keep.tile([P, PACK, N], F32, name="w2_raw")
         theta_sb = keep.tile([P, 4], F32, name="theta_sb")
 
-        def load_scales(queue, table, scales):
-            queue.dma_start(out=table[:].bitcast(I32)[0:P:8, :], in_=scales[0].bitcast(I32))
+        def load_scales(queue, table, scales, base):
+            queue.dma_start(out=table[:].bitcast(I32)[base : base + 16, :], in_=scales[0].bitcast(I32))
 
-        def place_scales(queue, plane, picked):
-            for r in range(4):
-                queue.dma_start(out=plane[:].bitcast(I32)[r:P:32, :], in_=picked[:].bitcast(I32)[8 * r : P : 32, :])
+        def place_scales(queues, plane, picked, base, quadrants):
+            for queue, q in zip(queues, quadrants):
+                queue.dma_start(
+                    out=plane[:].bitcast(I32)[32 * q : 32 * q + 4, :],
+                    in_=picked[:].bitcast(I32)[base + 4 * q : base + 4 * q + 4, :],
+                )
+
 
         def load_words(queue, table, words, lo, hi):
             queue.dma_start(out=table[:, lo:hi], in_=words[0].rearrange("p c r -> p (c r)").bitcast(I32)[:, lo:hi])
@@ -51,19 +55,20 @@ def tile_picked_ylatt_tanh_p_kernel(
         def load_weight(queue, raw, w):
             queue.dma_start(out=raw[:], in_=w.rearrange("(p j) n -> p j n", j=PACK))
 
-        nc.vector.memset(x_scale_table[:].bitcast(I32), 0)
         nc.gpsimd.memset(e_scale_table[:].bitcast(I32), 0)
+        nc.vector.memset(x_scale_table[:].bitcast(I32)[0:96, :], 0)
+        nc.vector.memset(x_scale_table[:].bitcast(I32)[96:112, :], 0)
         x_plane = keep.tile([P, S], U8, name="x_plane", align_bytes=64)
         e_plane = keep.tile([P, S], U8, name="e_plane", align_bytes=64)
         nc.vector.memset(x_plane[:].bitcast(I32), 0)
         nc.vector.memset(e_plane[:].bitcast(I32), 0)
         nc.scalar.dma_start(out=theta_sb[:], in_=theta)
+        load_weight(nc.scalar, w1_raw, w1)
         nc.sync.dma_start(offs_sb[:], offs)
+        load_scales(nc.sync, x_scale_table, x_scales, 112)
         nc.sync.dma_start(item_sb[:], item)
-        load_scales(nc.sync, x_scale_table, x_scales)
-        load_scales(nc.sync, e_scale_table, e_scales)
+        load_scales(nc.sync, e_scale_table, e_scales, 0)
         load_words(nc.sync, x_word_table, x_words, 0, T)
-        load_weight(nc.sync, w1_raw, w1)
         load_weight(nc.sync, w2_raw, w2)
         load_words(nc.sync, e_word_table, e_words, 0, W)
 
@@ -81,8 +86,8 @@ def tile_picked_ylatt_tanh_p_kernel(
             nc.scalar.activation(grouped[:], raw[:].rearrange("p j n -> p n j"), ACT.Identity)
             return grouped
 
-        def quantise(grouped, name):
-            codes = keep.tile([P, N], U32, name=name + "_codes", align_bytes=64)
+        def quantise(grouped, name, tag):
+            codes = keep.tile([P, N], U32, name=name + "_codes", tag=tag, align_bytes=64)
             scales = keep.tile([P, N], U8, name=name + "_scales", align_bytes=64)
             nc.vector.quantize_mx(
                 out=codes[:].bitcast(FP8X4), scales=scales[:], in_=grouped[:].rearrange("p n j -> p (n j)")
@@ -93,15 +98,21 @@ def tile_picked_ylatt_tanh_p_kernel(
         w2_grouped = group_weight(w2_raw, "w2_grouped", "w2_grouped")
 
         x_scale_picked = keep.tile([P, S], U8, name="x_scale_picked", align_bytes=64)
-        x_word_picked = keep.tile([P, S], U32, name="x_word_picked", align_bytes=64)
         e_scale_picked = keep.tile([P, S], U8, name="e_scale_picked", align_bytes=64)
         nc.vector.tensor_copy(x_scale_picked[:], x_scale_table[:].indirect(offs_sb[:]))
-        place_scales(nc.scalar, x_plane, x_scale_picked)
+        place_scales([nc.scalar] * 4, x_plane, x_scale_picked, 112, range(4))
         nc.vector.tensor_copy(e_scale_picked[:], e_scale_table[:].indirect(item_sb[:]))
-        place_scales(nc.sync, e_plane, e_scale_picked)
-        nc.vector.tensor_copy(x_word_picked[:], x_word_table[:].bitcast(U32).indirect(offs_sb[:]))
-        w1_codes, w1_scales = quantise(w1_grouped, "w1")
-        w2_codes, w2_scales = quantise(w2_grouped, "w2")
+        place_scales([nc.sync] * 3, e_plane, e_scale_picked, 0, range(1, 4))
+        w1_codes, w1_scales = quantise(w1_grouped, "w1", "held")
+        nc.vector.tensor_copy(e_plane[:].bitcast(I32)[0:32, :], e_scale_picked[:].bitcast(I32)[0:32, :])
+        x_picked = []
+        for lo in range(0, S, HALF):
+            picked = keep.tile([P, HALF], U32, name="x_word_picked%d" % lo, align_bytes=64)
+            nc.vector.tensor_copy(
+                picked[:], x_word_table[:].bitcast(U32).indirect(offs_sb[:, lo // 16 : (lo + HALF) // 16])
+            )
+            x_picked.append(picked)
+        w2_codes, w2_scales = quantise(w2_grouped, "w2", "w2_codes")
 
         a_tanh = keep.tile([N, S], F32, name="a_tanh")
         slope = keep.tile([N, S], F32, name="slope")
@@ -111,13 +122,13 @@ def tile_picked_ylatt_tanh_p_kernel(
                 out=a_sums[:],
                 lhsT=w1_codes[:].bitcast(FP8X4),
                 lhsT_scale=w1_scales[:],
-                rhs=x_word_picked[:, lo : lo + HALF].bitcast(FP8X4),
+                rhs=x_picked[lo // HALF][:].bitcast(FP8X4),
                 rhs_scale=x_plane[:, lo : lo + HALF],
                 start=True,
                 stop=True,
             )
             nc.scalar.activation(a_tanh[:, lo : lo + HALF], a_sums[:], ACT.Tanh, scale=0.5)
-            nc.scalar.activation(slope[:, lo : lo + HALF], a_tanh[:, lo : lo + HALF], ACT.Identity, scale=c_ab, bias=c_b)
+        nc.scalar.activation(slope[:, 0:HALF], a_tanh[:, 0:HALF], ACT.Identity, scale=c_ab, bias=c_b)
 
         b_tanh = []
         for h in range(2):
@@ -141,6 +152,7 @@ def tile_picked_ylatt_tanh_p_kernel(
                 nc.scalar.activation(b_piece[:], b_sums[:], ACT.Tanh, scale=0.5)
                 b_tanh.append(b_piece)
 
+        nc.vector.tensor_scalar(slope[:, HALF:S], a_tanh[:, HALF:S], c_ab, c_b, ALU.mult, ALU.add)
         for pair in range(0, S // PIECE, 2):
             products = []
             for i in (pair, pair + 1):

@@ -16,7 +16,8 @@ P = 128
 PACK = 4
 K, T, S, N, W = 512, 1024, 512, 128, 2048
 HALF = S // 2
-PIECE = 128
+PIECES = ((0, 128), (128, 256), (256, 384), (384, 512))
+TOP = P - 16
 FLOPS = 2 * 2 * K * N * S
 
 
@@ -32,8 +33,10 @@ def tile_picked_ylatt_tanh_p_kernel(
         item_sb = keep.tile([P, S // 16], U16, name="item_sb")
         x_word_table = keep.tile([P, T], I32, name="x_word_table", align_bytes=64)
         e_word_table = keep.tile([P, W], I32, name="e_word_table", align_bytes=64)
-        x_scale_table = keep.tile([P, T], U8, name="x_scale_table", align_bytes=64)
-        e_scale_table = keep.tile([P, W], U8, name="e_scale_table", tag="held", align_bytes=64)
+        x_scale_table = keep.tile([P, T], U8, name="x_scale_table", tag="held", align_bytes=64)
+        e_scale_table = keep.tile([P, W], U8, name="e_scale_table", align_bytes=64)
+        x_plane = keep.tile([P, S], U8, name="x_plane", align_bytes=64)
+        e_plane = keep.tile([P, S], U8, name="e_plane", align_bytes=64)
         w1_raw = keep.tile([P, PACK, N], F32, name="w1_raw")
         w2_raw = keep.tile([P, PACK, N], F32, name="w2_raw")
         theta_sb = keep.tile([P, 4], F32, name="theta_sb")
@@ -41,36 +44,33 @@ def tile_picked_ylatt_tanh_p_kernel(
         def load_scales(queue, table, scales, base):
             queue.dma_start(out=table[:].bitcast(I32)[base : base + 16, :], in_=scales[0].bitcast(I32))
 
-        def place_scales(queues, plane, picked, base, quadrants):
-            for queue, q in zip(queues, quadrants):
+        def place_scales(queue, plane, picked, base, quadrants):
+            for q in quadrants:
                 queue.dma_start(
                     out=plane[:].bitcast(I32)[32 * q : 32 * q + 4, :],
                     in_=picked[:].bitcast(I32)[base + 4 * q : base + 4 * q + 4, :],
                 )
 
-
-        def load_words(queue, table, words, lo, hi):
-            queue.dma_start(out=table[:, lo:hi], in_=words[0].rearrange("p c r -> p (c r)").bitcast(I32)[:, lo:hi])
+        def load_words(queue, table, words):
+            queue.dma_start(out=table[:], in_=words[0].rearrange("p c r -> p (c r)").bitcast(I32))
 
         def load_weight(queue, raw, w):
             queue.dma_start(out=raw[:], in_=w.rearrange("(p j) n -> p j n", j=PACK))
 
-        nc.gpsimd.memset(e_scale_table[:].bitcast(I32), 0)
-        nc.vector.memset(x_scale_table[:].bitcast(I32)[0:96, :], 0)
-        nc.vector.memset(x_scale_table[:].bitcast(I32)[96:112, :], 0)
-        x_plane = keep.tile([P, S], U8, name="x_plane", align_bytes=64)
-        e_plane = keep.tile([P, S], U8, name="e_plane", align_bytes=64)
-        nc.vector.memset(x_plane[:].bitcast(I32), 0)
+        nc.vector.memset(x_scale_table[:].bitcast(I32), 0)
+        nc.vector.memset(e_scale_table[:].bitcast(I32)[0:96, :], 0)
+        nc.gpsimd.memset(e_scale_table[:].bitcast(I32)[96:TOP, :], 0)
         nc.vector.memset(e_plane[:].bitcast(I32), 0)
+        nc.vector.memset(x_plane[:].bitcast(I32), 0)
         nc.scalar.dma_start(out=theta_sb[:], in_=theta)
-        load_weight(nc.scalar, w1_raw, w1)
-        nc.sync.dma_start(offs_sb[:], offs)
-        load_scales(nc.sync, x_scale_table, x_scales, 112)
+        load_scales(nc.scalar, e_scale_table, e_scales, TOP)
         nc.sync.dma_start(item_sb[:], item)
-        load_scales(nc.sync, e_scale_table, e_scales, 0)
-        load_words(nc.sync, x_word_table, x_words, 0, T)
+        nc.sync.dma_start(offs_sb[:], offs)
         load_weight(nc.sync, w2_raw, w2)
-        load_words(nc.sync, e_word_table, e_words, 0, W)
+        load_scales(nc.sync, x_scale_table, x_scales, 0)
+        load_words(nc.sync, e_word_table, e_words)
+        load_weight(nc.sync, w1_raw, w1)
+        load_words(nc.sync, x_word_table, x_words)
 
         terms = keep.tile([P, 5, 4], F32, name="terms")
         coef = keep.tile([P, 5], F32, name="coef")
@@ -81,8 +81,8 @@ def tile_picked_ylatt_tanh_p_kernel(
         nc.scalar.activation(terms[:, 3, 0:2], theta_sb[:, 2:4], ACT.Identity, scale=0.5, bias=shift, accum_out=c_b)
         nc.scalar.activation(terms[:, 4, 0:2], theta_sb[:, 0:4:3], ACT.Identity, scale=0.5, bias=shift, accum_out=c_ab)
 
-        def group_weight(raw, name, tag):
-            grouped = keep.tile([P, N, PACK], BF16, name=name, tag=tag, align_bytes=64)
+        def group_weight(raw, name):
+            grouped = keep.tile([P, N, PACK], BF16, name=name, align_bytes=64)
             nc.scalar.activation(grouped[:], raw[:].rearrange("p j n -> p n j"), ACT.Identity)
             return grouped
 
@@ -94,75 +94,66 @@ def tile_picked_ylatt_tanh_p_kernel(
             )
             return codes, scales
 
-        w1_grouped = group_weight(w1_raw, "w1_grouped", "w1_grouped")
-        w2_grouped = group_weight(w2_raw, "w2_grouped", "w2_grouped")
+        def gather_words(table, offsets, lo, hi, name):
+            picked = keep.tile([P, hi - lo], U32, name=name, align_bytes=64)
+            nc.vector.tensor_copy(picked[:], table[:].bitcast(U32).indirect(offsets[:, lo // 16 : hi // 16]))
+            return picked
 
-        x_scale_picked = keep.tile([P, S], U8, name="x_scale_picked", align_bytes=64)
-        e_scale_picked = keep.tile([P, S], U8, name="e_scale_picked", align_bytes=64)
-        nc.vector.tensor_copy(x_scale_picked[:], x_scale_table[:].indirect(offs_sb[:]))
-        place_scales([nc.scalar] * 4, x_plane, x_scale_picked, 112, range(4))
-        nc.vector.tensor_copy(e_scale_picked[:], e_scale_table[:].indirect(item_sb[:]))
-        place_scales([nc.sync] * 3, e_plane, e_scale_picked, 0, range(1, 4))
-        w1_codes, w1_scales = quantise(w1_grouped, "w1", "held")
-        nc.vector.tensor_copy(e_plane[:].bitcast(I32)[0:32, :], e_scale_picked[:].bitcast(I32)[0:32, :])
-        x_picked = []
-        for lo in range(0, S, HALF):
-            picked = keep.tile([P, HALF], U32, name="x_word_picked%d" % lo, align_bytes=64)
-            nc.vector.tensor_copy(
-                picked[:], x_word_table[:].bitcast(U32).indirect(offs_sb[:, lo // 16 : (lo + HALF) // 16])
-            )
-            x_picked.append(picked)
-        w2_codes, w2_scales = quantise(w2_grouped, "w2", "w2_codes")
-
-        a_tanh = keep.tile([N, S], F32, name="a_tanh")
-        slope = keep.tile([N, S], F32, name="slope")
-        for lo in range(0, S, HALF):
-            a_sums = psum.tile([N, HALF], F32, name="a_sums%d" % lo)
+        def product_mx(codes, scales, picked, plane, lo, hi, name):
+            sums = psum.tile([N, hi - lo], F32, name=name)
             nc.tensor.matmul_mx(
-                out=a_sums[:],
-                lhsT=w1_codes[:].bitcast(FP8X4),
-                lhsT_scale=w1_scales[:],
-                rhs=x_picked[lo // HALF][:].bitcast(FP8X4),
-                rhs_scale=x_plane[:, lo : lo + HALF],
+                out=sums[:],
+                lhsT=codes[:].bitcast(FP8X4),
+                lhsT_scale=scales[:],
+                rhs=picked[:].bitcast(FP8X4),
+                rhs_scale=plane[:, lo:hi],
                 start=True,
                 stop=True,
             )
-            nc.scalar.activation(a_tanh[:, lo : lo + HALF], a_sums[:], ACT.Tanh, scale=0.5)
-        nc.scalar.activation(slope[:, 0:HALF], a_tanh[:, 0:HALF], ACT.Identity, scale=c_ab, bias=c_b)
+            return sums
 
-        b_tanh = []
-        for h in range(2):
-            picked = keep.tile([P, HALF], U32, name="e_word_picked%d" % h, align_bytes=64)
-            nc.vector.tensor_copy(
-                picked[:], e_word_table[:].bitcast(U32).indirect(item_sb[:, h * HALF // 16 : (h + 1) * HALF // 16])
-            )
-            for u in range(HALF // PIECE):
-                first = h * HALF + u * PIECE
-                b_sums = psum.tile([N, PIECE], F32, name="b_sums%d" % first)
-                nc.tensor.matmul_mx(
-                    out=b_sums[:],
-                    lhsT=w2_codes[:].bitcast(FP8X4),
-                    lhsT_scale=w2_scales[:],
-                    rhs=picked[:, u * PIECE : (u + 1) * PIECE].bitcast(FP8X4),
-                    rhs_scale=e_plane[:, first : first + PIECE],
-                    start=True,
-                    stop=True,
-                )
-                b_piece = keep.tile([N, PIECE], F32, name="b_tanh%d" % first)
-                nc.scalar.activation(b_piece[:], b_sums[:], ACT.Tanh, scale=0.5)
-                b_tanh.append(b_piece)
+        w2_grouped = group_weight(w2_raw, "w2_grouped")
+        x_scale_picked = keep.tile([P, S], U8, name="x_scale_picked", align_bytes=64)
+        e_scale_picked = keep.tile([P, S], U8, name="e_scale_picked", align_bytes=64)
+        nc.vector.tensor_copy(e_scale_picked[:], e_scale_table[:].indirect(item_sb[:]))
+        place_scales(nc.scalar, e_plane, e_scale_picked, TOP, range(4))
+        nc.vector.tensor_copy(x_scale_picked[:], x_scale_table[:].indirect(offs_sb[:]))
+        place_scales(nc.sync, x_plane, x_scale_picked, 0, range(1, 4))
+        w2_codes, w2_scales = quantise(w2_grouped, "w2", "held")
+        nc.vector.tensor_copy(x_plane[:].bitcast(I32)[0:32, :], x_scale_picked[:].bitcast(I32)[0:32, :])
+        w1_grouped = group_weight(w1_raw, "w1_grouped")
 
-        nc.vector.tensor_scalar(slope[:, HALF:S], a_tanh[:, HALF:S], c_ab, c_b, ALU.mult, ALU.add)
-        for pair in range(0, S // PIECE, 2):
+        b_tanh = keep.tile([N, S], F32, name="b_tanh")
+        slope = keep.tile([N, S], F32, name="slope")
+        for lo in range(0, S, HALF):
+            hi = lo + HALF
+            picked = gather_words(e_word_table, item_sb, lo, hi, "e_word_picked%d" % lo)
+            b_sums = product_mx(w2_codes, w2_scales, picked, e_plane, lo, hi, "b_sums%d" % lo)
+            nc.scalar.activation(b_tanh[:, lo:hi], b_sums[:], ACT.Tanh, scale=0.5)
+        nc.scalar.activation(slope[:, 0:HALF], b_tanh[:, 0:HALF], ACT.Identity, scale=c_ab, bias=c_a)
+
+        w1_codes, w1_scales = quantise(w1_grouped, "w1", "w1_codes")
+
+        a_tanh = []
+        for lo, hi in PIECES:
+            picked = gather_words(x_word_table, offs_sb, lo, hi, "x_word_picked%d" % lo)
+            a_sums = product_mx(w1_codes, w1_scales, picked, x_plane, lo, hi, "a_sums%d" % lo)
+            a_piece = keep.tile([N, hi - lo], F32, name="a_tanh%d" % lo)
+            nc.scalar.activation(a_piece[:], a_sums[:], ACT.Tanh, scale=0.5)
+            a_tanh.append(a_piece)
+        nc.vector.tensor_scalar(slope[:, HALF:S], b_tanh[:, HALF:S], c_ab, c_a, ALU.mult, ALU.add)
+
+        for pair in range(0, len(PIECES), 2):
             products = []
-            for i in (pair, pair + 1):
-                product = keep.tile([N, PIECE], F32, name="product%d" % i)
-                nc.vector.tensor_tensor(product[:], b_tanh[i][:], slope[:, i * PIECE : (i + 1) * PIECE], ALU.mult)
+            for i in range(pair, min(pair + 2, len(PIECES))):
+                lo, hi = PIECES[i]
+                product = keep.tile([N, hi - lo], F32, name="product%d" % i)
+                nc.vector.tensor_tensor(product[:], a_tanh[i][:], slope[:, lo:hi], ALU.mult)
                 products.append(product)
-            for i in (pair, pair + 1):
-                cols = slice(i * PIECE, (i + 1) * PIECE)
-                lattice = keep.tile([N, PIECE], F32, name="lattice%d" % i)
-                result = keep.tile([N, PIECE], F32, name="result%d" % i)
-                nc.vector.scalar_tensor_tensor(lattice[:], a_tanh[:, cols], c_a, products[i - pair][:], ALU.mult, ALU.add)
+            for i in range(pair, min(pair + 2, len(PIECES))):
+                lo, hi = PIECES[i]
+                lattice = keep.tile([N, hi - lo], F32, name="lattice%d" % i)
+                result = keep.tile([N, hi - lo], F32, name="result%d" % i)
+                nc.vector.scalar_tensor_tensor(lattice[:], b_tanh[:, lo:hi], c_b, products[i - pair][:], ALU.mult, ALU.add)
                 nc.scalar.activation(result[:], lattice[:], ACT.Tanh, bias=c_one)
-                nc.sync.dma_start(out=out[:, cols], in_=result[:])
+                nc.sync.dma_start(out=out[:, lo:hi], in_=result[:])

@@ -59,14 +59,14 @@ def tile_picked_ylatt_tanh_p_kernel(
 
         nc.vector.memset(x_scale_table[:].bitcast(I32), 0)
         nc.vector.memset(e_scale_table[:].bitcast(I32)[0:96, :], 0)
-        nc.gpsimd.memset(e_scale_table[:].bitcast(I32)[96:TOP, :], 0)
+        nc.vector.memset(e_scale_table[:].bitcast(I32)[96:TOP, :], 0)
         nc.vector.memset(e_plane[:].bitcast(I32), 0)
         nc.vector.memset(x_plane[:].bitcast(I32), 0)
         nc.scalar.dma_start(out=theta_sb[:], in_=theta)
-        load_scales(nc.scalar, e_scale_table, e_scales, TOP)
+        load_weight(nc.scalar, w2_raw, w2)
         nc.sync.dma_start(item_sb[:], item)
+        load_scales(nc.sync, e_scale_table, e_scales, TOP)
         nc.sync.dma_start(offs_sb[:], offs)
-        load_weight(nc.sync, w2_raw, w2)
         load_scales(nc.sync, x_scale_table, x_scales, 0)
         load_words(nc.sync, e_word_table, e_words)
         load_weight(nc.sync, w1_raw, w1)

@@ -18,6 +18,7 @@ K, T, S, N, W = 512, 1024, 512, 128, 2048
 HALF = S // 2
 PIECES = ((0, 128), (128, 256), (256, 384), (384, 512))
 TOP = P - 16
+X_FRONT = 640
 FLOPS = 2 * 2 * K * N * S
 
 
@@ -41,18 +42,18 @@ def tile_picked_ylatt_tanh_p_kernel(
         w2_raw = keep.tile([P, PACK, N], F32, name="w2_raw")
         theta_sb = keep.tile([P, 4], F32, name="theta_sb")
 
-        def load_scales(queue, table, scales, base):
-            queue.dma_start(out=table[:].bitcast(I32)[base : base + 16, :], in_=scales[0].bitcast(I32))
+        def load_scales(queue, table, scales, base, first, count):
+            queue.dma_start(
+                out=table[:].bitcast(I32)[base : base + count, :], in_=scales[0].bitcast(I32)[first : first + count, :]
+            )
 
-        def place_scales(queue, plane, picked, base, quadrants):
-            for q in quadrants:
-                queue.dma_start(
-                    out=plane[:].bitcast(I32)[32 * q : 32 * q + 4, :],
-                    in_=picked[:].bitcast(I32)[base + 4 * q : base + 4 * q + 4, :],
-                )
+        def place_scales(queue, plane, picked, source, q):
+            queue.dma_start(
+                out=plane[:].bitcast(I32)[32 * q : 32 * q + 4, :], in_=picked[:].bitcast(I32)[source : source + 4, :]
+            )
 
-        def load_words(queue, table, words):
-            queue.dma_start(out=table[:], in_=words[0].rearrange("p c r -> p (c r)").bitcast(I32))
+        def load_words(queue, table, words, lo, hi):
+            queue.dma_start(out=table[:, lo:hi], in_=words[0].rearrange("p c r -> p (c r)").bitcast(I32)[:, lo:hi])
 
         def load_weight(queue, raw, w):
             queue.dma_start(out=raw[:], in_=w.rearrange("(p j) n -> p j n", j=PACK))
@@ -61,16 +62,16 @@ def tile_picked_ylatt_tanh_p_kernel(
         nc.vector.memset(e_scale_table[:].bitcast(I32)[0:96, :], 0)
         nc.vector.memset(e_scale_table[:].bitcast(I32)[96:TOP, :], 0)
         nc.vector.memset(e_plane[:].bitcast(I32), 0)
-        nc.vector.memset(x_plane[:].bitcast(I32), 0)
-        nc.scalar.dma_start(out=theta_sb[:], in_=theta)
+        load_scales(nc.scalar, e_scale_table, e_scales, TOP, 0, 16)
         load_weight(nc.scalar, w2_raw, w2)
+        nc.scalar.dma_start(out=theta_sb[:], in_=theta)
         nc.sync.dma_start(item_sb[:], item)
-        load_scales(nc.sync, e_scale_table, e_scales, TOP)
         nc.sync.dma_start(offs_sb[:], offs)
-        load_scales(nc.sync, x_scale_table, x_scales, 0)
-        load_words(nc.sync, e_word_table, e_words)
+        load_scales(nc.sync, x_scale_table, x_scales, 28, 0, 8)
+        load_scales(nc.sync, x_scale_table, x_scales, 92, 8, 8)
+        load_words(nc.sync, e_word_table, e_words, 0, W)
         load_weight(nc.sync, w1_raw, w1)
-        load_words(nc.sync, x_word_table, x_words)
+        load_words(nc.sync, x_word_table, x_words, 0, X_FRONT)
 
         terms = keep.tile([P, 5, 4], F32, name="terms")
         coef = keep.tile([P, 5], F32, name="coef")
@@ -116,11 +117,14 @@ def tile_picked_ylatt_tanh_p_kernel(
         x_scale_picked = keep.tile([P, S], U8, name="x_scale_picked", align_bytes=64)
         e_scale_picked = keep.tile([P, S], U8, name="e_scale_picked", align_bytes=64)
         nc.vector.tensor_copy(e_scale_picked[:], e_scale_table[:].indirect(item_sb[:]))
-        place_scales(nc.scalar, e_plane, e_scale_picked, TOP, range(4))
+        for q in range(4):
+            place_scales(nc.sync, e_plane, e_scale_picked, TOP + 4 * q, q)
+        load_words(nc.sync, x_word_table, x_words, X_FRONT, T)
         nc.vector.tensor_copy(x_scale_picked[:], x_scale_table[:].indirect(offs_sb[:]))
-        place_scales(nc.sync, x_plane, x_scale_picked, 0, range(1, 4))
         w2_codes, w2_scales = quantise(w2_grouped, "w2", "held")
-        nc.vector.tensor_copy(x_plane[:].bitcast(I32)[0:32, :], x_scale_picked[:].bitcast(I32)[0:32, :])
+        nc.vector.tensor_copy(x_plane[:].bitcast(I32), x_scale_picked[:].bitcast(I32))
+        place_scales(nc.sync, x_plane, x_scale_picked, 28, 0)
+        place_scales(nc.sync, x_plane, x_scale_picked, 92, 2)
         w1_grouped = group_weight(w1_raw, "w1_grouped")
 
         b_tanh = keep.tile([N, S], F32, name="b_tanh")
@@ -130,7 +134,7 @@ def tile_picked_ylatt_tanh_p_kernel(
             picked = gather_words(e_word_table, item_sb, lo, hi, "e_word_picked%d" % lo)
             b_sums = product_mx(w2_codes, w2_scales, picked, e_plane, lo, hi, "b_sums%d" % lo)
             nc.scalar.activation(b_tanh[:, lo:hi], b_sums[:], ACT.Tanh, scale=0.5)
-        nc.scalar.activation(slope[:, 0:HALF], b_tanh[:, 0:HALF], ACT.Identity, scale=c_ab, bias=c_a)
+            nc.scalar.activation(slope[:, lo:hi], b_tanh[:, lo:hi], ACT.Identity, scale=c_ab, bias=c_a)
 
         w1_codes, w1_scales = quantise(w1_grouped, "w1", "w1_codes")
 
@@ -141,7 +145,6 @@ def tile_picked_ylatt_tanh_p_kernel(
             a_piece = keep.tile([N, hi - lo], F32, name="a_tanh%d" % lo)
             nc.scalar.activation(a_piece[:], a_sums[:], ACT.Tanh, scale=0.5)
             a_tanh.append(a_piece)
-        nc.vector.tensor_scalar(slope[:, HALF:S], b_tanh[:, HALF:S], c_ab, c_a, ALU.mult, ALU.add)
 
         for pair in range(0, len(PIECES), 2):
             products = []

@@ -134,7 +134,7 @@ def tile_picked_ylatt_tanh_p_kernel(
             picked = gather_words(e_word_table, item_sb, lo, hi, "e_word_picked%d" % lo)
             b_sums = product_mx(w2_codes, w2_scales, picked, e_plane, lo, hi, "b_sums%d" % lo)
             nc.scalar.activation(b_tanh[:, lo:hi], b_sums[:], ACT.Tanh, scale=0.5)
-            nc.scalar.activation(slope[:, lo:hi], b_tanh[:, lo:hi], ACT.Identity, scale=c_ab, bias=c_a)
+        nc.scalar.activation(slope[:, 0:HALF], b_tanh[:, 0:HALF], ACT.Identity, scale=c_ab, bias=c_a)
 
         w1_codes, w1_scales = quantise(w1_grouped, "w1", "w1_codes")
 
@@ -145,6 +145,7 @@ def tile_picked_ylatt_tanh_p_kernel(
             a_piece = keep.tile([N, hi - lo], F32, name="a_tanh%d" % lo)
             nc.scalar.activation(a_piece[:], a_sums[:], ACT.Tanh, scale=0.5)
             a_tanh.append(a_piece)
+        nc.vector.tensor_scalar(slope[:, HALF:S], b_tanh[:, HALF:S], c_ab, c_a, ALU.mult, ALU.add)
 
         for pair in range(0, len(PIECES), 2):
             products = []

@@ -14,6 +14,7 @@ ACT = mybir.ActivationFunctionType
 
 P = 128
 PACK = 4
+QUADRANT = 32
 K, T, S, N, W = 512, 1024, 512, 128, 2048
 HALF = S // 2
 PIECES = ((0, 128), (128, 256), (256, 384), (384, 512))
@@ -37,23 +38,19 @@ def tile_picked_ylatt_tanh_p_kernel(
         x_scale_table = keep.tile([P, T], U8, name="x_scale_table", tag="held", align_bytes=64)
         e_scale_table = keep.tile([P, W], U8, name="e_scale_table", align_bytes=64)
         x_plane = keep.tile([P, S], U8, name="x_plane", align_bytes=64)
+        e_scale_picked = keep.tile([P, S], U8, name="e_scale_picked", align_bytes=64)
         e_plane = keep.tile([P, S], U8, name="e_plane", align_bytes=64)
         w1_raw = keep.tile([P, PACK, N], F32, name="w1_raw")
         w2_raw = keep.tile([P, PACK, N], F32, name="w2_raw")
         theta_sb = keep.tile([P, 4], F32, name="theta_sb")
 
-        def load_scales(queue, table, scales, base, first, count):
+        def load_x_scale_rows(queue, r):
             queue.dma_start(
-                out=table[:].bitcast(I32)[base : base + count, :], in_=scales[0].bitcast(I32)[first : first + count, :]
+                out=x_scale_table[:].bitcast(I32)[r:P:QUADRANT, :], in_=x_scales[0].bitcast(I32)[r:16:4, :]
             )
 
-        def place_scales(queue, plane, picked, source, q):
-            queue.dma_start(
-                out=plane[:].bitcast(I32)[32 * q : 32 * q + 4, :], in_=picked[:].bitcast(I32)[source : source + 4, :]
-            )
-
-        def load_words(queue, table, words, lo, hi):
-            queue.dma_start(out=table[:, lo:hi], in_=words[0].rearrange("p c r -> p (c r)").bitcast(I32)[:, lo:hi])
+        def load_words(table, words, lo, hi):
+            nc.sync.dma_start(out=table[:, lo:hi], in_=words[0].rearrange("p c r -> p (c r)").bitcast(I32)[:, lo:hi])
 
         def load_weight(queue, raw, w):
             queue.dma_start(out=raw[:], in_=w.rearrange("(p j) n -> p j n", j=PACK))
@@ -62,25 +59,18 @@ def tile_picked_ylatt_tanh_p_kernel(
         nc.vector.memset(e_scale_table[:].bitcast(I32)[0:96, :], 0)
         nc.vector.memset(e_scale_table[:].bitcast(I32)[96:TOP, :], 0)
         nc.vector.memset(e_plane[:].bitcast(I32), 0)
-        load_scales(nc.scalar, e_scale_table, e_scales, TOP, 0, 16)
-        load_weight(nc.scalar, w2_raw, w2)
-        nc.scalar.dma_start(out=theta_sb[:], in_=theta)
+        nc.scalar.dma_start(out=e_scale_table[:].bitcast(I32)[TOP:P, :], in_=e_scales[0].bitcast(I32))
         nc.sync.dma_start(item_sb[:], item)
         nc.sync.dma_start(offs_sb[:], offs)
-        load_scales(nc.sync, x_scale_table, x_scales, 28, 0, 8)
-        load_scales(nc.sync, x_scale_table, x_scales, 92, 8, 8)
-        load_words(nc.sync, e_word_table, e_words, 0, W)
+        load_x_scale_rows(nc.scalar, 0)
+        load_x_scale_rows(nc.scalar, 1)
+        load_x_scale_rows(nc.sync, 2)
+        load_x_scale_rows(nc.sync, 3)
+        load_weight(nc.gpsimd, w2_raw, w2)
+        nc.gpsimd.dma_start(out=theta_sb[:], in_=theta)
+        load_words(e_word_table, e_words, 0, W)
         load_weight(nc.sync, w1_raw, w1)
-        load_words(nc.sync, x_word_table, x_words, 0, X_FRONT)
-
-        terms = keep.tile([P, 5, 4], F32, name="terms")
-        coef = keep.tile([P, 5], F32, name="coef")
-        c_one, c_a, c_b, c_ab, shift = (coef[:, i : i + 1] for i in range(5))
-        nc.scalar.activation(terms[:, 0, :], theta_sb[:], ACT.Identity, scale=-0.125, accum_out=shift)
-        nc.scalar.activation(terms[:, 1, :], theta_sb[:], ACT.Identity, scale=0.25, accum_out=c_one)
-        nc.scalar.activation(terms[:, 2, 0:2], theta_sb[:, 1:4:2], ACT.Identity, scale=0.5, bias=shift, accum_out=c_a)
-        nc.scalar.activation(terms[:, 3, 0:2], theta_sb[:, 2:4], ACT.Identity, scale=0.5, bias=shift, accum_out=c_b)
-        nc.scalar.activation(terms[:, 4, 0:2], theta_sb[:, 0:4:3], ACT.Identity, scale=0.5, bias=shift, accum_out=c_ab)
+        load_words(x_word_table, x_words, 0, X_FRONT)
 
         def group_weight(raw, name):
             grouped = keep.tile([P, N, PACK], BF16, name=name, align_bytes=64)
@@ -114,17 +104,25 @@ def tile_picked_ylatt_tanh_p_kernel(
             return sums
 
         w2_grouped = group_weight(w2_raw, "w2_grouped")
-        x_scale_picked = keep.tile([P, S], U8, name="x_scale_picked", align_bytes=64)
-        e_scale_picked = keep.tile([P, S], U8, name="e_scale_picked", align_bytes=64)
+
+        terms = keep.tile([P, 5, 4], F32, name="terms")
+        coef = keep.tile([P, 5], F32, name="coef")
+        c_one, c_a, c_b, c_ab, shift = (coef[:, i : i + 1] for i in range(5))
+        nc.scalar.activation(terms[:, 0, :], theta_sb[:], ACT.Identity, scale=-0.125, accum_out=shift)
+        nc.scalar.activation(terms[:, 1, :], theta_sb[:], ACT.Identity, scale=0.25, accum_out=c_one)
+        nc.scalar.activation(terms[:, 2, 0:2], theta_sb[:, 1:4:2], ACT.Identity, scale=0.5, bias=shift, accum_out=c_a)
+        nc.scalar.activation(terms[:, 3, 0:2], theta_sb[:, 2:4], ACT.Identity, scale=0.5, bias=shift, accum_out=c_b)
+        nc.scalar.activation(terms[:, 4, 0:2], theta_sb[:, 0:4:3], ACT.Identity, scale=0.5, bias=shift, accum_out=c_ab)
+
         nc.vector.tensor_copy(e_scale_picked[:], e_scale_table[:].indirect(item_sb[:]))
         for q in range(4):
-            place_scales(nc.sync, e_plane, e_scale_picked, TOP + 4 * q, q)
-        load_words(nc.sync, x_word_table, x_words, X_FRONT, T)
-        nc.vector.tensor_copy(x_scale_picked[:], x_scale_table[:].indirect(offs_sb[:]))
+            nc.sync.dma_start(
+                out=e_plane[:].bitcast(I32)[QUADRANT * q : QUADRANT * q + 4, :],
+                in_=e_scale_picked[:].bitcast(I32)[TOP + 4 * q : TOP + 4 * q + 4, :],
+            )
+        load_words(x_word_table, x_words, X_FRONT, T)
+        nc.vector.tensor_copy(x_plane[:], x_scale_table[:].indirect(offs_sb[:]))
         w2_codes, w2_scales = quantise(w2_grouped, "w2", "held")
-        nc.vector.tensor_copy(x_plane[:].bitcast(I32), x_scale_picked[:].bitcast(I32))
-        place_scales(nc.sync, x_plane, x_scale_picked, 28, 0)
-        place_scales(nc.sync, x_plane, x_scale_picked, 92, 2)
         w1_grouped = group_weight(w1_raw, "w1_grouped")
 
         b_tanh = keep.tile([N, S], F32, name="b_tanh")
@@ -147,17 +145,23 @@ def tile_picked_ylatt_tanh_p_kernel(
             a_tanh.append(a_piece)
         nc.vector.tensor_scalar(slope[:, HALF:S], b_tanh[:, HALF:S], c_ab, c_a, ALU.mult, ALU.add)
 
-        for pair in range(0, len(PIECES), 2):
-            products = []
-            for i in range(pair, min(pair + 2, len(PIECES))):
-                lo, hi = PIECES[i]
-                product = keep.tile([N, hi - lo], F32, name="product%d" % i)
-                nc.vector.tensor_tensor(product[:], a_tanh[i][:], slope[:, lo:hi], ALU.mult)
-                products.append(product)
-            for i in range(pair, min(pair + 2, len(PIECES))):
-                lo, hi = PIECES[i]
-                lattice = keep.tile([N, hi - lo], F32, name="lattice%d" % i)
-                result = keep.tile([N, hi - lo], F32, name="result%d" % i)
-                nc.vector.scalar_tensor_tensor(lattice[:], b_tanh[:, lo:hi], c_b, products[i - pair][:], ALU.mult, ALU.add)
-                nc.scalar.activation(result[:], lattice[:], ACT.Tanh, bias=c_one)
-                nc.sync.dma_start(out=out[:, lo:hi], in_=result[:])
+        def multiply(i):
+            lo, hi = PIECES[i]
+            product = keep.tile([N, hi - lo], F32, name="product%d" % i)
+            nc.vector.tensor_tensor(product[:], a_tanh[i][:], slope[:, lo:hi], ALU.mult)
+            return product
+
+        def finish(i, product):
+            lo, hi = PIECES[i]
+            lattice = keep.tile([N, hi - lo], F32, name="lattice%d" % i)
+            result = keep.tile([N, hi - lo], F32, name="result%d" % i)
+            nc.vector.scalar_tensor_tensor(lattice[:], b_tanh[:, lo:hi], c_b, product[:], ALU.mult, ALU.add)
+            nc.scalar.activation(result[:], lattice[:], ACT.Tanh, bias=c_one)
+            nc.sync.dma_start(out=out[:, lo:hi], in_=result[:])
+
+        waiting = multiply(0)
+        for i in range(1, len(PIECES)):
+            ahead = multiply(i)
+            finish(i - 1, waiting)
+            waiting = ahead
+        finish(len(PIECES) - 1, waiting)

@@ -18,6 +18,7 @@ QUADRANT = 32
 K, T, S, N, W = 512, 1024, 512, 128, 2048
 HALF = S // 2
 PIECES = ((0, 128), (128, 256), (256, 384), (384, 512))
+X_GATHERS = ((0, 256), (256, 384), (384, 512))
 TOP = P - 16
 X_FRONT = 640
 FLOPS = 2 * 2 * K * N * S
@@ -35,18 +36,19 @@ def tile_picked_ylatt_tanh_p_kernel(
         item_sb = keep.tile([P, S // 16], U16, name="item_sb")
         x_word_table = keep.tile([P, T], I32, name="x_word_table", align_bytes=64)
         e_word_table = keep.tile([P, W], I32, name="e_word_table", align_bytes=64)
-        x_scale_table = keep.tile([P, T], U8, name="x_scale_table", tag="held", align_bytes=64)
+        x_scale_table = keep.tile([P, T], U8, name="x_scale_table", align_bytes=64)
         e_scale_table = keep.tile([P, W], U8, name="e_scale_table", align_bytes=64)
-        x_plane = keep.tile([P, S], U8, name="x_plane", align_bytes=64)
+        x_scale_picked = keep.tile([P, S], U8, name="x_scale_picked", align_bytes=64)
         e_scale_picked = keep.tile([P, S], U8, name="e_scale_picked", align_bytes=64)
         e_plane = keep.tile([P, S], U8, name="e_plane", align_bytes=64)
         w1_raw = keep.tile([P, PACK, N], F32, name="w1_raw")
-        w2_raw = keep.tile([P, PACK, N], F32, name="w2_raw")
+        w2_raw = keep.tile([P, PACK, N], F32, name="w2_raw", tag="held", align_bytes=64)
         theta_sb = keep.tile([P, 4], F32, name="theta_sb")
 
-        def load_x_scale_rows(queue, r):
+        def load_x_scale_rows(queue, base, first, count):
             queue.dma_start(
-                out=x_scale_table[:].bitcast(I32)[r:P:QUADRANT, :], in_=x_scales[0].bitcast(I32)[r:16:4, :]
+                out=x_scale_table[:].bitcast(I32)[base : base + count, :],
+                in_=x_scales[0].bitcast(I32)[first : first + count, :],
             )
 
         def load_words(table, words, lo, hi):
@@ -62,12 +64,10 @@ def tile_picked_ylatt_tanh_p_kernel(
         nc.scalar.dma_start(out=e_scale_table[:].bitcast(I32)[TOP:P, :], in_=e_scales[0].bitcast(I32))
         nc.sync.dma_start(item_sb[:], item)
         nc.sync.dma_start(offs_sb[:], offs)
-        load_x_scale_rows(nc.scalar, 0)
-        load_x_scale_rows(nc.scalar, 1)
-        load_x_scale_rows(nc.sync, 2)
-        load_x_scale_rows(nc.sync, 3)
-        load_weight(nc.gpsimd, w2_raw, w2)
-        nc.gpsimd.dma_start(out=theta_sb[:], in_=theta)
+        load_weight(nc.scalar, w2_raw, w2)
+        nc.scalar.dma_start(out=theta_sb[:], in_=theta)
+        load_x_scale_rows(nc.sync, 28, 0, 8)
+        load_x_scale_rows(nc.sync, 92, 8, 8)
         load_words(e_word_table, e_words, 0, W)
         load_weight(nc.sync, w1_raw, w1)
         load_words(x_word_table, x_words, 0, X_FRONT)
@@ -96,7 +96,7 @@ def tile_picked_ylatt_tanh_p_kernel(
                 out=sums[:],
                 lhsT=codes[:].bitcast(FP8X4),
                 lhsT_scale=scales[:],
-                rhs=picked[:].bitcast(FP8X4),
+                rhs=picked.bitcast(FP8X4),
                 rhs_scale=plane[:, lo:hi],
                 start=True,
                 stop=True,
@@ -121,8 +121,12 @@ def tile_picked_ylatt_tanh_p_kernel(
                 in_=e_scale_picked[:].bitcast(I32)[TOP + 4 * q : TOP + 4 * q + 4, :],
             )
         load_words(x_word_table, x_words, X_FRONT, T)
-        nc.vector.tensor_copy(x_plane[:], x_scale_table[:].indirect(offs_sb[:]))
-        w2_codes, w2_scales = quantise(w2_grouped, "w2", "held")
+        nc.vector.tensor_copy(x_scale_picked[:], x_scale_table[:].indirect(offs_sb[:]))
+        w2_codes, w2_scales = quantise(w2_grouped, "w2", "w2_codes")
+        x_plane = keep.tile([P, S], U8, name="x_plane", tag="held", align_bytes=64)
+        nc.vector.tensor_copy(x_plane[:].bitcast(I32), x_scale_picked[:].bitcast(I32))
+        nc.sync.dma_start(out=x_plane[:].bitcast(I32)[0:4, :], in_=x_scale_picked[:].bitcast(I32)[28:32, :])
+        nc.sync.dma_start(out=x_plane[:].bitcast(I32)[64:68, :], in_=x_scale_picked[:].bitcast(I32)[92:96, :])
         w1_grouped = group_weight(w1_raw, "w1_grouped")
 
         b_tanh = keep.tile([N, S], F32, name="b_tanh")
@@ -130,19 +134,22 @@ def tile_picked_ylatt_tanh_p_kernel(
         for lo in range(0, S, HALF):
             hi = lo + HALF
             picked = gather_words(e_word_table, item_sb, lo, hi, "e_word_picked%d" % lo)
-            b_sums = product_mx(w2_codes, w2_scales, picked, e_plane, lo, hi, "b_sums%d" % lo)
+            b_sums = product_mx(w2_codes, w2_scales, picked[:], e_plane, lo, hi, "b_sums%d" % lo)
             nc.scalar.activation(b_tanh[:, lo:hi], b_sums[:], ACT.Tanh, scale=0.5)
         nc.scalar.activation(slope[:, 0:HALF], b_tanh[:, 0:HALF], ACT.Identity, scale=c_ab, bias=c_a)
 
         w1_codes, w1_scales = quantise(w1_grouped, "w1", "w1_codes")
 
         a_tanh = []
-        for lo, hi in PIECES:
-            picked = gather_words(x_word_table, offs_sb, lo, hi, "x_word_picked%d" % lo)
-            a_sums = product_mx(w1_codes, w1_scales, picked, x_plane, lo, hi, "a_sums%d" % lo)
-            a_piece = keep.tile([N, hi - lo], F32, name="a_tanh%d" % lo)
-            nc.scalar.activation(a_piece[:], a_sums[:], ACT.Tanh, scale=0.5)
-            a_tanh.append(a_piece)
+        for first, end in X_GATHERS:
+            picked = gather_words(x_word_table, offs_sb, first, end, "x_word_picked%d" % first)
+            for lo, hi in PIECES:
+                if first <= lo < end:
+                    words = picked[:, lo - first : hi - first]
+                    a_sums = product_mx(w1_codes, w1_scales, words, x_plane, lo, hi, "a_sums%d" % lo)
+                    a_piece = keep.tile([N, hi - lo], F32, name="a_tanh%d" % lo)
+                    nc.scalar.activation(a_piece[:], a_sums[:], ACT.Tanh, scale=0.5)
+                    a_tanh.append(a_piece)
         nc.vector.tensor_scalar(slope[:, HALF:S], b_tanh[:, HALF:S], c_ab, c_a, ALU.mult, ALU.add)
 
         def multiply(i):

from contextlib import ExitStack

import concourse.mybir as mybir

F32 = mybir.dt.float32
BF16 = mybir.dt.bfloat16
I32 = mybir.dt.int32
U32 = mybir.dt.uint32
U16 = mybir.dt.uint16
U8 = mybir.dt.uint8
FP8X4 = mybir.dt.float8_e4m3fn_x4
ALU = mybir.AluOpType
ACT = mybir.ActivationFunctionType

P = 128
PACK = 4
QUADRANT = 32
K, T, S, N, W = 512, 1024, 512, 128, 2048
HALF = S // 2
PIECES = ((0, 128), (128, 256), (256, 384), (384, 512))
X_GATHERS = ((0, 256), (256, 384), (384, 512))
TOP = P - 16
X_FRONT = 640
FLOPS = 2 * 2 * K * N * S


def tile_picked_ylatt_tanh_p_kernel(
    tc, x_words, x_scales, e_words, e_scales, w1, w2, theta, offs, item, out
):
    nc = tc.nc
    with ExitStack() as ctx:
        keep = ctx.enter_context(tc.tile_pool(name="keep", bufs=1))
        psum = ctx.enter_context(tc.psum_pool(name="psum", bufs=1))

        offs_sb = keep.tile([P, S // 16], U16, name="offs_sb")
        item_sb = keep.tile([P, S // 16], U16, name="item_sb")
        x_word_table = keep.tile([P, T], I32, name="x_word_table", align_bytes=64)
        e_word_table = keep.tile([P, W], I32, name="e_word_table", align_bytes=64)
        x_scale_table = keep.tile([P, T], U8, name="x_scale_table", align_bytes=64)
        e_scale_table = keep.tile([P, W], U8, name="e_scale_table", align_bytes=64)
        x_scale_picked = keep.tile([P, S], U8, name="x_scale_picked", align_bytes=64)
        e_scale_picked = keep.tile([P, S], U8, name="e_scale_picked", align_bytes=64)
        e_plane = keep.tile([P, S], U8, name="e_plane", align_bytes=64)
        w1_raw = keep.tile([P, PACK, N], F32, name="w1_raw")
        w2_raw = keep.tile([P, PACK, N], F32, name="w2_raw", tag="held", align_bytes=64)
        theta_sb = keep.tile([P, 4], F32, name="theta_sb")

        def load_x_scale_rows(queue, base, first, count):
            queue.dma_start(
                out=x_scale_table[:].bitcast(I32)[base : base + count, :],
                in_=x_scales[0].bitcast(I32)[first : first + count, :],
            )

        def load_words(table, words, lo, hi):
            nc.sync.dma_start(out=table[:, lo:hi], in_=words[0].rearrange("p c r -> p (c r)").bitcast(I32)[:, lo:hi])

        def load_weight(queue, raw, w):
            queue.dma_start(out=raw[:], in_=w.rearrange("(p j) n -> p j n", j=PACK))

        nc.vector.memset(x_scale_table[:].bitcast(I32), 0)
        nc.vector.memset(e_scale_table[:].bitcast(I32)[0:96, :], 0)
        nc.vector.memset(e_scale_table[:].bitcast(I32)[96:TOP, :], 0)
        nc.vector.memset(e_plane[:].bitcast(I32), 0)
        nc.scalar.dma_start(out=e_scale_table[:].bitcast(I32)[TOP:P, :], in_=e_scales[0].bitcast(I32))
        nc.sync.dma_start(item_sb[:], item)
        nc.sync.dma_start(offs_sb[:], offs)
        load_weight(nc.scalar, w2_raw, w2)
        nc.scalar.dma_start(out=theta_sb[:], in_=theta)
        load_x_scale_rows(nc.sync, 28, 0, 8)
        load_x_scale_rows(nc.sync, 92, 8, 8)
        load_words(e_word_table, e_words, 0, W)
        load_weight(nc.sync, w1_raw, w1)
        load_words(x_word_table, x_words, 0, X_FRONT)

        def group_weight(raw, name):
            grouped = keep.tile([P, N, PACK], BF16, name=name, align_bytes=64)
            nc.scalar.activation(grouped[:], raw[:].rearrange("p j n -> p n j"), ACT.Identity)
            return grouped

        def quantise(grouped, name, tag):
            codes = keep.tile([P, N], U32, name=name + "_codes", tag=tag, align_bytes=64)
            scales = keep.tile([P, N], U8, name=name + "_scales", align_bytes=64)
            nc.vector.quantize_mx(
                out=codes[:].bitcast(FP8X4), scales=scales[:], in_=grouped[:].rearrange("p n j -> p (n j)")
            )
            return codes, scales

        def gather_words(table, offsets, lo, hi, name):
            picked = keep.tile([P, hi - lo], U32, name=name, align_bytes=64)
            nc.vector.tensor_copy(picked[:], table[:].bitcast(U32).indirect(offsets[:, lo // 16 : hi // 16]))
            return picked

        def product_mx(codes, scales, picked, plane, lo, hi, name):
            sums = psum.tile([N, hi - lo], F32, name=name)
            nc.tensor.matmul_mx(
                out=sums[:],
                lhsT=codes[:].bitcast(FP8X4),
                lhsT_scale=scales[:],
                rhs=picked.bitcast(FP8X4),
                rhs_scale=plane[:, lo:hi],
                start=True,
                stop=True,
            )
            return sums

        w2_grouped = group_weight(w2_raw, "w2_grouped")

        terms = keep.tile([P, 5, 4], F32, name="terms")
        coef = keep.tile([P, 5], F32, name="coef")
        c_one, c_a, c_b, c_ab, shift = (coef[:, i : i + 1] for i in range(5))
        nc.scalar.activation(terms[:, 0, :], theta_sb[:], ACT.Identity, scale=-0.125, accum_out=shift)
        nc.scalar.activation(terms[:, 1, :], theta_sb[:], ACT.Identity, scale=0.25, accum_out=c_one)
        nc.scalar.activation(terms[:, 2, 0:2], theta_sb[:, 1:4:2], ACT.Identity, scale=0.5, bias=shift, accum_out=c_a)
        nc.scalar.activation(terms[:, 3, 0:2], theta_sb[:, 2:4], ACT.Identity, scale=0.5, bias=shift, accum_out=c_b)
        nc.scalar.activation(terms[:, 4, 0:2], theta_sb[:, 0:4:3], ACT.Identity, scale=0.5, bias=shift, accum_out=c_ab)

        nc.vector.tensor_copy(e_scale_picked[:], e_scale_table[:].indirect(item_sb[:]))
        for q in range(4):
            nc.sync.dma_start(
                out=e_plane[:].bitcast(I32)[QUADRANT * q : QUADRANT * q + 4, :],
                in_=e_scale_picked[:].bitcast(I32)[TOP + 4 * q : TOP + 4 * q + 4, :],
            )
        load_words(x_word_table, x_words, X_FRONT, T)
        nc.vector.tensor_copy(x_scale_picked[:], x_scale_table[:].indirect(offs_sb[:]))
        w2_codes, w2_scales = quantise(w2_grouped, "w2", "w2_codes")
        x_plane = keep.tile([P, S], U8, name="x_plane", tag="held", align_bytes=64)
        nc.vector.tensor_copy(x_plane[:].bitcast(I32), x_scale_picked[:].bitcast(I32))
        nc.sync.dma_start(out=x_plane[:].bitcast(I32)[0:4, :], in_=x_scale_picked[:].bitcast(I32)[28:32, :])
        nc.sync.dma_start(out=x_plane[:].bitcast(I32)[64:68, :], in_=x_scale_picked[:].bitcast(I32)[92:96, :])
        w1_grouped = group_weight(w1_raw, "w1_grouped")

        b_tanh = keep.tile([N, S], F32, name="b_tanh")
        slope = keep.tile([N, S], F32, name="slope")
        for lo in range(0, S, HALF):
            hi = lo + HALF
            picked = gather_words(e_word_table, item_sb, lo, hi, "e_word_picked%d" % lo)
            b_sums = product_mx(w2_codes, w2_scales, picked[:], e_plane, lo, hi, "b_sums%d" % lo)
            nc.scalar.activation(b_tanh[:, lo:hi], b_sums[:], ACT.Tanh, scale=0.5)
        nc.scalar.activation(slope[:, 0:HALF], b_tanh[:, 0:HALF], ACT.Identity, scale=c_ab, bias=c_a)

        w1_codes, w1_scales = quantise(w1_grouped, "w1", "w1_codes")

        a_tanh = []
        for first, end in X_GATHERS:
            picked = gather_words(x_word_table, offs_sb, first, end, "x_word_picked%d" % first)
            for lo, hi in PIECES:
                if first <= lo < end:
                    words = picked[:, lo - first : hi - first]
                    a_sums = product_mx(w1_codes, w1_scales, words, x_plane, lo, hi, "a_sums%d" % lo)
                    a_piece = keep.tile([N, hi - lo], F32, name="a_tanh%d" % lo)
                    nc.scalar.activation(a_piece[:], a_sums[:], ACT.Tanh, scale=0.5)
                    a_tanh.append(a_piece)
        nc.vector.tensor_scalar(slope[:, HALF:S], b_tanh[:, HALF:S], c_ab, c_a, ALU.mult, ALU.add)

        def multiply(i):
            lo, hi = PIECES[i]
            product = keep.tile([N, hi - lo], F32, name="product%d" % i)
            nc.vector.tensor_tensor(product[:], a_tanh[i][:], slope[:, lo:hi], ALU.mult)
            return product

        def finish(i, product):
            lo, hi = PIECES[i]
            lattice = keep.tile([N, hi - lo], F32, name="lattice%d" % i)
            result = keep.tile([N, hi - lo], F32, name="result%d" % i)
            nc.vector.scalar_tensor_tensor(lattice[:], b_tanh[:, lo:hi], c_b, product[:], ALU.mult, ALU.add)
            nc.scalar.activation(result[:], lattice[:], ACT.Tanh, bias=c_one)
            nc.sync.dma_start(out=out[:, lo:hi], in_=result[:])

        waiting = multiply(0)
        for i in range(1, len(PIECES)):
            ahead = multiply(i)
            finish(i - 1, waiting)
            waiting = ahead
        finish(len(PIECES) - 1, waiting)
